import numpy as np
CORES = [72,74,76,78,200,202,204,206,328,330,332,334,456,458,460,462]
N = 16
def setup_inputs(rng):
    return {"x": rng.standard_normal((N, 128, 256), dtype=np.float32)}
def reference(x):
    b = 256 // N
    blocks = x.reshape(N, 128, N, b)
    return {"y": np.ascontiguousarray(blocks.transpose(2, 1, 0, 3)).reshape(N, 128, 256)}

@@ -1,0 +1,153 @@
+from concourse.bass import DstId, RemoteDMATransfer
+
+SCRATCH = {
+    "slots": ("dram", [4, 128, 16], "float32"),
+}
+SEMAPHORES = ["a", "c0", "c1"]
+
+
+def _bits(mask):
+    return [1 << i for i in range(mask.bit_length()) if (mask >> i) & 1]
+
+
+def rank_program(g, core, T, topo):
+    rank = T.rank_of(core)
+    if rank is None:
+        return
+    cores = list(T.cores)
+    b = T.x.shape[1] // len(cores)
+    S = T.slots
+    A = T.sem.a
+    C = [T.sem.c0, T.sem.c1]
+    queues = (g.sync, g.scalar)
+
+    byhost = {}
+    for k in cores:
+        byhost.setdefault(topo.host(k), []).append(k)
+    n = len(byhost[topo.host(core)])
+
+    def around(h):
+        rep = byhost[h][0]
+        near = [o for o in byhost if o != h and topo.may_write(rep, byhost[o][0])]
+        same = [o for o in near if topo.rack(o) == topo.rack(h)]
+        far = [o for o in near if topo.rack(o) != topo.rack(h)]
+        return same[0], far[0]
+
+    h = topo.host(core)
+    c = byhost[h].index(core)
+    HX, HY = around(h)
+    diag = [o for o in byhost if o not in (h, HX, HY)][0]
+
+    def xb(k):
+        j = T.rank_of(k)
+        return T.x[:, j * b:(j + 1) * b]
+
+    def yb(k):
+        j = T.rank_of(k)
+        return T.y[:, j * b:(j + 1) * b]
+
+    def shares(dsts):
+        m = topo.mask(core, dsts[0])
+        for d in dsts:
+            m &= topo.mask(core, d)
+        bits = _bits(m)
+        per = 1
+        while per * 2 * len(dsts) <= len(bits):
+            per *= 2
+        return per, [sum(bits[i * per:(i + 1) * per]) for i in range(len(dsts))]
+
+    def send(moves, rsem, lsem):
+        per, masks = shares([d for _, d, _ in moves])
+        trs = []
+        for (s, d, t), m in zip(moves, masks):
+            rid, pid = topo.addr(d, core)
+            trs.append(RemoteDMATransfer(dst_ids=[DstId(rid=rid, pnc=pid)], dma_engine_mask=m, remote_sem=rsem,
+                                         src=S[s], dst=S[t]))
+        g.remote_dma_fused(trs, local_sem=lsem)
+        return per
+
+    def signal(dsts, sem):
+        per, masks = shares(dsts)
+        trs = []
+        for d, m in zip(dsts, masks):
+            rid, pid = topo.addr(d, core)
+            trs.append(RemoteDMATransfer(dst_ids=[DstId(rid=rid, pnc=pid)], dma_engine_mask=m, remote_sem=sem))
+        g.remote_dma_fused(trs, local_sem=sem)
+        return per
+
+    def on(d):
+        return byhost[h][(c + d) % n]
+
+    def via(i, hr):
+        k = sorted((HX, HY)).index(hr)
+        cv = c ^ (i + 2 * k)
+        return byhost[hr][c if h < diag else cv], byhost[diag][cv]
+
+    def relayed(i):
+        k = sorted(around(HX)).index(h)
+        lo, hi = c, c ^ (i + 2 * k)
+        return (byhost[HX][lo], byhost[HY][hi]) if HX < HY else (byhost[HX][hi], byhost[HY][lo])
+
+    rounds = []
+    for t in range(n):
+        pr = (byhost[HX][c ^ t], byhost[HY][c ^ t])
+        rounds.append(("D", pr, pr, None))
+    for i in range(2):
+        (wx, vx), (wy, vy) = via(i, HX), via(i, HY)
+        rounds.append(("H", (wx, wy), (vx, vy), relayed(i)))
+    partners = byhost[HX] + byhost[HY]
+
+    cc = [0, 0]
+    g.sync.dma_start(S[0], xb(on(1))).then_inc(C[0], 16)
+    g.scalar.dma_start(S[1], xb(on(2))).then_inc(C[0], 16)
+    g.scalar.dma_start(yb(core), xb(core)).then_inc(C[1], 16)
+    cc[0] += 32
+    cc[1] += 16
+    g.wait_ge(C[0], cc[0])
+    a = 4 * send([(0, on(1), 2), (1, on(2), 3)], A, A)
+    g.sync.wait_ge(A, a)
+    g.scalar.wait_ge(A, a)
+    g.sync.dma_start(S[1], xb(on(3))).then_inc(A, 16)
+    g.scalar.dma_start(yb(on(-1)), S[2]).then_inc(A, 16)
+    g.sync.dma_start(yb(on(2)), S[3]).then_inc(A, 16)
+    a += 48
+    g.wait_ge(A, a)
+    m = topo.mask(core, on(3))
+    rid, pid = topo.addr(on(3), core)
+    g.remote_dma(S[0], S[1], C[0], C[0], pid, rid, m)
+    cc[0] += 2 * len(_bits(m))
+    Ss, Rs = [2, 3], [0, 1]
+    for q, k in zip(queues, (0, 1)):
+        q.wait_ge(A, a)
+        q.dma_start(S[Ss[k]], xb(rounds[0][2][k])).then_inc(C[1], 16)
+    cc[1] += 32
+    g.scalar.wait_ge(C[0], cc[0])
+    g.scalar.dma_start(yb(on(1)), S[0]).then_inc(A, 16)
+    a += 16
+    g.wait_ge(C[0], cc[0])
+    g.wait_ge(A, a)
+
+    for idx, (kind, tgt, blk, fwd) in enumerate(rounds):
+        p = (idx + 1) % 2
+        nxt = rounds[idx + 1][2] if idx + 1 < len(rounds) else None
+        cc[p] += 2 * len(partners) * signal(partners, C[p])
+        g.wait_ge(C[p], cc[p])
+        a += 4 * send([(Ss[0], tgt[0], Rs[0]), (Ss[1], tgt[1], Rs[1])], A, A)
+        if kind == "D":
+            full, free, gate, level = Rs, Ss, A, a
+        else:
+            g.wait_ge(A, a)
+            cc[p] += 4 * send([(Rs[0], fwd[1], Ss[1]), (Rs[1], fwd[0], Ss[0])], C[p], C[p])
+            full, free, gate, level = Ss, Rs, C[p], cc[p]
+        for q, k in zip(queues, (0, 1)):
+            q.wait_ge(gate, level)
+            q.dma_start(yb(blk[k]), S[full[k]]).then_inc(A, 16)
+            if nxt:
+                q.dma_start(S[free[k]], xb(nxt[k])).then_inc(C[1 - p], 16)
+        a += 32
+        if nxt:
+            cc[1 - p] += 32
+        if kind == "H":
+            g.wait_ge(C[p], cc[p])
+            Ss, Rs = Rs, Ss
+        g.wait_ge(A, a)

@@ -5,6 +5,9 @@ SCRATCH = {
 }
 SEMAPHORES = ["a", "c0", "c1"]
 
+MX = ((0, 1), (2, 3))
+MY = ((0, 2), (3, 1))
+
 
 def _bits(mask):
     return [1 << i for i in range(mask.bit_length()) if (mask >> i) & 1]
@@ -17,8 +20,8 @@ def rank_program(g, core, T, topo):
     cores = list(T.cores)
     b = T.x.shape[1] // len(cores)
     S = T.slots
-    A = T.sem.a
-    C = [T.sem.c0, T.sem.c1]
+    sem = {"a": T.sem.a, 0: T.sem.c0, 1: T.sem.c1}
+    lv = {"a": 0, 0: 0, 1: 0}
     queues = (g.sync, g.scalar)
 
     byhost = {}
@@ -26,17 +29,23 @@ def rank_program(g, core, T, topo):
         byhost.setdefault(topo.host(k), []).append(k)
     n = len(byhost[topo.host(core)])
 
-    def around(h):
-        rep = byhost[h][0]
-        near = [o for o in byhost if o != h and topo.may_write(rep, byhost[o][0])]
-        same = [o for o in near if topo.rack(o) == topo.rack(h)]
-        far = [o for o in near if topo.rack(o) != topo.rack(h)]
+    def around(hh):
+        rep = byhost[hh][0]
+        near = [o for o in byhost if o != hh and topo.may_write(rep, byhost[o][0])]
+        same = [o for o in near if topo.rack(o) == topo.rack(hh)]
+        far = [o for o in near if topo.rack(o) != topo.rack(hh)]
         return same[0], far[0]
 
     h = topo.host(core)
     c = byhost[h].index(core)
     HX, HY = around(h)
     diag = [o for o in byhost if o not in (h, HX, HY)][0]
+    h0 = min(byhost)
+
+    def mu(route, hh, i):
+        if route == 0:
+            return MX[0 if hh in (h0, around(h0)[1]) else 1][i]
+        return MY[0 if topo.rack(hh) == topo.rack(h0) else 1][i]
 
     def xb(k):
         j = T.rank_of(k)
@@ -56,98 +65,91 @@ def rank_program(g, core, T, topo):
             per *= 2
         return per, [sum(bits[i * per:(i + 1) * per]) for i in range(len(dsts))]
 
-    def send(moves, rsem, lsem):
+    def send(moves, s):
         per, masks = shares([d for _, d, _ in moves])
         trs = []
-        for (s, d, t), m in zip(moves, masks):
+        for (src, d, dst), m in zip(moves, masks):
             rid, pid = topo.addr(d, core)
-            trs.append(RemoteDMATransfer(dst_ids=[DstId(rid=rid, pnc=pid)], dma_engine_mask=m, remote_sem=rsem,
-                                         src=S[s], dst=S[t]))
-        g.remote_dma_fused(trs, local_sem=lsem)
-        return per
+            trs.append(RemoteDMATransfer(dst_ids=[DstId(rid=rid, pnc=pid)], dma_engine_mask=m, remote_sem=sem[s],
+                                         src=S[src], dst=S[dst]))
+        g.remote_dma_fused(trs, local_sem=sem[s])
+        lv[s] += 2 * per * len(moves)
 
-    def signal(dsts, sem):
+    def signal(dsts, s):
         per, masks = shares(dsts)
         trs = []
         for d, m in zip(dsts, masks):
             rid, pid = topo.addr(d, core)
-            trs.append(RemoteDMATransfer(dst_ids=[DstId(rid=rid, pnc=pid)], dma_engine_mask=m, remote_sem=sem))
-        g.remote_dma_fused(trs, local_sem=sem)
-        return per
+            trs.append(RemoteDMATransfer(dst_ids=[DstId(rid=rid, pnc=pid)], dma_engine_mask=m, remote_sem=sem[s]))
+        g.remote_dma_fused(trs, local_sem=sem[s])
+        lv[s] += 2 * per * len(dsts)
+
+    def turn(s, slots, came, go):
+        for q, k in zip(queues, (0, 1)):
+            q.wait_ge(sem[s], lv[s])
+            q.dma_start(yb(came[k]), S[slots[k]]).then_inc(sem[s], 16)
+        lv[s] += 32
+        for q, k in zip(queues, (0, 1)):
+            q.wait_ge(sem[s], lv[s])
+            q.dma_start(S[slots[k]], xb(go[k])).then_inc(sem[s], 16)
+        lv[s] += 32
+        g.wait_ge(sem[s], lv[s])
 
     def on(d):
         return byhost[h][(c + d) % n]
 
-    def via(i, hr):
-        k = sorted((HX, HY)).index(hr)
-        cv = c ^ (i + 2 * k)
-        return byhost[hr][c if h < diag else cv], byhost[diag][cv]
-
-    def relayed(i):
-        k = sorted(around(HX)).index(h)
-        lo, hi = c, c ^ (i + 2 * k)
-        return (byhost[HX][lo], byhost[HY][hi]) if HX < HY else (byhost[HX][hi], byhost[HY][lo])
-
-    rounds = []
-    for t in range(n):
-        pr = (byhost[HX][c ^ t], byhost[HY][c ^ t])
-        rounds.append(("D", pr, pr, None))
+    plan = []
     for i in range(2):
-        (wx, vx), (wy, vy) = via(i, HX), via(i, HY)
-        rounds.append(("H", (wx, wy), (vx, vy), relayed(i)))
+        w = (byhost[HX][c ^ mu(0, h, i)], byhost[HY][c ^ mu(1, h, i)])
+        v = (byhost[diag][c ^ mu(0, h, i) ^ mu(1, diag, i)], byhost[diag][c ^ mu(1, h, i) ^ mu(0, diag, i)])
+        u = (byhost[HX][c ^ mu(0, HX, i)], byhost[HY][c ^ mu(1, HY, i)])
+        plan.append((w, v, u))
     partners = byhost[HX] + byhost[HY]
 
-    cc = [0, 0]
-    g.sync.dma_start(S[0], xb(on(1))).then_inc(C[0], 16)
-    g.scalar.dma_start(S[1], xb(on(2))).then_inc(C[0], 16)
-    g.scalar.dma_start(yb(core), xb(core)).then_inc(C[1], 16)
-    cc[0] += 32
-    cc[1] += 16
-    g.wait_ge(C[0], cc[0])
-    a = 4 * send([(0, on(1), 2), (1, on(2), 3)], A, A)
-    g.sync.wait_ge(A, a)
-    g.scalar.wait_ge(A, a)
-    g.sync.dma_start(S[1], xb(on(3))).then_inc(A, 16)
-    g.scalar.dma_start(yb(on(-1)), S[2]).then_inc(A, 16)
-    g.sync.dma_start(yb(on(2)), S[3]).then_inc(A, 16)
-    a += 48
-    g.wait_ge(A, a)
-    m = topo.mask(core, on(3))
-    rid, pid = topo.addr(on(3), core)
-    g.remote_dma(S[0], S[1], C[0], C[0], pid, rid, m)
-    cc[0] += 2 * len(_bits(m))
-    Ss, Rs = [2, 3], [0, 1]
+    g.sync.dma_start(S[0], xb(on(1))).then_inc(sem[0], 16)
+    g.scalar.dma_start(S[1], xb(on(2))).then_inc(sem[0], 16)
+    g.scalar.dma_start(yb(core), xb(core)).then_inc(sem[1], 16)
+    lv[0] += 32
+    lv[1] += 16
+    g.wait_ge(sem[0], lv[0])
+    send([(0, on(1), 2), (1, on(2), 3)], "a")
+    g.sync.wait_ge(sem["a"], lv["a"])
+    g.scalar.wait_ge(sem["a"], lv["a"])
+    g.sync.dma_start(S[1], xb(on(3))).then_inc(sem["a"], 16)
+    g.scalar.dma_start(yb(on(-1)), S[2]).then_inc(sem["a"], 16)
+    g.sync.dma_start(yb(on(2)), S[3]).then_inc(sem["a"], 16)
+    lv["a"] += 48
+    g.wait_ge(sem["a"], lv["a"])
+    send([(1, on(3), 0)], 0)
+    E, F = [2, 3], [0, 1]
     for q, k in zip(queues, (0, 1)):
-        q.wait_ge(A, a)
-        q.dma_start(S[Ss[k]], xb(rounds[0][2][k])).then_inc(C[1], 16)
-    cc[1] += 32
-    g.scalar.wait_ge(C[0], cc[0])
-    g.scalar.dma_start(yb(on(1)), S[0]).then_inc(A, 16)
-    a += 16
-    g.wait_ge(C[0], cc[0])
-    g.wait_ge(A, a)
+        q.wait_ge(sem["a"], lv["a"])
+        q.dma_start(S[E[k]], xb(plan[0][1][k])).then_inc(sem[1], 16)
+    lv[1] += 32
+    g.scalar.wait_ge(sem[0], lv[0])
+    g.scalar.dma_start(yb(on(1)), S[0]).then_inc(sem["a"], 16)
+    lv["a"] += 16
+    g.wait_ge(sem[0], lv[0])
+    g.wait_ge(sem["a"], lv["a"])
 
-    for idx, (kind, tgt, blk, fwd) in enumerate(rounds):
-        p = (idx + 1) % 2
-        nxt = rounds[idx + 1][2] if idx + 1 < len(rounds) else None
-        cc[p] += 2 * len(partners) * signal(partners, C[p])
-        g.wait_ge(C[p], cc[p])
-        a += 4 * send([(Ss[0], tgt[0], Rs[0]), (Ss[1], tgt[1], Rs[1])], A, A)
-        if kind == "D":
-            full, free, gate, level = Rs, Ss, A, a
-        else:
-            g.wait_ge(A, a)
-            cc[p] += 4 * send([(Rs[0], fwd[1], Ss[1]), (Rs[1], fwd[0], Ss[0])], C[p], C[p])
-            full, free, gate, level = Ss, Rs, C[p], cc[p]
+    for i, (w, v, u) in enumerate(plan):
+        p = 1 - i
+        signal(partners, p)
+        g.wait_ge(sem[p], lv[p])
+        send([(E[0], w[0], F[0]), (E[1], w[1], F[1])], "a")
+        g.wait_ge(sem["a"], lv["a"])
+        send([(F[0], u[1], E[1]), (F[1], u[0], E[0])], p)
+        turn(p, E, v, w)
+        send([(E[0], w[0], F[1]), (E[1], w[1], F[0])], "a")
+        turn("a", (F[1], F[0]), u, u)
+        send([(F[1], u[0], E[0]), (F[0], u[1], E[1])], p)
         for q, k in zip(queues, (0, 1)):
-            q.wait_ge(gate, level)
-            q.dma_start(yb(blk[k]), S[full[k]]).then_inc(A, 16)
-            if nxt:
-                q.dma_start(S[free[k]], xb(nxt[k])).then_inc(C[1 - p], 16)
-        a += 32
-        if nxt:
-            cc[1 - p] += 32
-        if kind == "H":
-            g.wait_ge(C[p], cc[p])
-            Ss, Rs = Rs, Ss
-        g.wait_ge(A, a)
+            q.wait_ge(sem[p], lv[p])
+            q.dma_start(yb(w[k]), S[E[k]]).then_inc(sem[p], 16)
+            if i + 1 < len(plan):
+                q.dma_start(S[F[k]], xb(plan[i + 1][1][k])).then_inc(sem[1 - p], 16)
+        lv[p] += 32
+        if i + 1 < len(plan):
+            lv[1 - p] += 32
+        g.wait_ge(sem[p], lv[p])
+        E, F = F, E

@@ -132,9 +132,9 @@ def rank_program(g, core, T, topo):
     g.wait_ge(sem[0], lv[0])
     g.wait_ge(sem["a"], lv["a"])
 
+    signal(partners, 1)
     for i, (w, v, u) in enumerate(plan):
         p = 1 - i
-        signal(partners, p)
         g.wait_ge(sem[p], lv[p])
         send([(E[0], w[0], F[0]), (E[1], w[1], F[1])], "a")
         g.wait_ge(sem["a"], lv["a"])
@@ -143,13 +143,13 @@ def rank_program(g, core, T, topo):
         send([(E[0], w[0], F[1]), (E[1], w[1], F[0])], "a")
         turn("a", (F[1], F[0]), u, u)
         send([(F[1], u[0], E[0]), (F[0], u[1], E[1])], p)
-        for q, k in zip(queues, (0, 1)):
-            q.wait_ge(sem[p], lv[p])
-            q.dma_start(yb(w[k]), S[E[k]]).then_inc(sem[p], 16)
-            if i + 1 < len(plan):
-                q.dma_start(S[F[k]], xb(plan[i + 1][1][k])).then_inc(sem[1 - p], 16)
-        lv[p] += 32
         if i + 1 < len(plan):
-            lv[1 - p] += 32
-        g.wait_ge(sem[p], lv[p])
-        E, F = F, E
+            g.wait_ge(sem[p], lv[p])
+            signal(list(plan[i + 1][2]), 1 - p)
+            turn(p, E, w, plan[i + 1][1])
+        else:
+            for q, k in zip(queues, (0, 1)):
+                q.wait_ge(sem[p], lv[p])
+                q.dma_start(yb(w[k]), S[E[k]]).then_inc(sem[p], 16)
+            lv[p] += 32
+            g.wait_ge(sem[p], lv[p])

@@ -104,24 +104,22 @@ def rank_program(g, core, T, topo):
         v = (byhost[diag][c ^ mu(0, h, i) ^ mu(1, diag, i)], byhost[diag][c ^ mu(1, h, i) ^ mu(0, diag, i)])
         u = (byhost[HX][c ^ mu(0, HX, i)], byhost[HY][c ^ mu(1, HY, i)])
         plan.append((w, v, u))
-    partners = byhost[HX] + byhost[HY]
 
+    E, F = [2, 3], [0, 1]
     g.sync.dma_start(S[0], xb(on(1))).then_inc(sem[0], 16)
     g.scalar.dma_start(S[1], xb(on(2))).then_inc(sem[0], 16)
-    g.scalar.dma_start(yb(core), xb(core)).then_inc(sem[1], 16)
     lv[0] += 32
-    lv[1] += 16
     g.wait_ge(sem[0], lv[0])
-    send([(0, on(1), 2), (1, on(2), 3)], "a")
+    send([(0, on(1), E[0]), (1, on(2), E[1])], "a")
     g.sync.wait_ge(sem["a"], lv["a"])
-    g.scalar.wait_ge(sem["a"], lv["a"])
     g.sync.dma_start(S[1], xb(on(3))).then_inc(sem["a"], 16)
-    g.scalar.dma_start(yb(on(-1)), S[2]).then_inc(sem["a"], 16)
-    g.sync.dma_start(yb(on(2)), S[3]).then_inc(sem["a"], 16)
-    lv["a"] += 48
+    lv["a"] += 16
     g.wait_ge(sem["a"], lv["a"])
     send([(1, on(3), 0)], 0)
-    E, F = [2, 3], [0, 1]
+    for q, k in zip(queues, (0, 1)):
+        q.wait_ge(sem["a"], lv["a"])
+        q.dma_start(yb((on(-1), on(2))[k]), S[E[k]]).then_inc(sem["a"], 16)
+    lv["a"] += 32
     for q, k in zip(queues, (0, 1)):
         q.wait_ge(sem["a"], lv["a"])
         q.dma_start(S[E[k]], xb(plan[0][1][k])).then_inc(sem[1], 16)
@@ -129,10 +127,12 @@ def rank_program(g, core, T, topo):
     g.scalar.wait_ge(sem[0], lv[0])
     g.scalar.dma_start(yb(on(1)), S[0]).then_inc(sem["a"], 16)
     lv["a"] += 16
+    g.scalar.dma_start(yb(core), xb(core)).then_inc(sem[1], 16)
+    lv[1] += 16
     g.wait_ge(sem[0], lv[0])
     g.wait_ge(sem["a"], lv["a"])
 
-    signal(partners, 1)
+    signal(list(plan[0][2]) + list(plan[1][0]), 1)
     for i, (w, v, u) in enumerate(plan):
         p = 1 - i
         g.wait_ge(sem[p], lv[p])

from concourse.bass import DstId, RemoteDMATransfer

SCRATCH = {
    "slots": ("dram", [4, 128, 16], "float32"),
}
SEMAPHORES = ["a", "c0", "c1"]

MX = ((0, 1), (2, 3))
MY = ((0, 2), (3, 1))


def _bits(mask):
    return [1 << i for i in range(mask.bit_length()) if (mask >> i) & 1]


def rank_program(g, core, T, topo):
    rank = T.rank_of(core)
    if rank is None:
        return
    cores = list(T.cores)
    b = T.x.shape[1] // len(cores)
    S = T.slots
    sem = {"a": T.sem.a, 0: T.sem.c0, 1: T.sem.c1}
    lv = {"a": 0, 0: 0, 1: 0}
    queues = (g.sync, g.scalar)

    byhost = {}
    for k in cores:
        byhost.setdefault(topo.host(k), []).append(k)
    n = len(byhost[topo.host(core)])

    def around(hh):
        rep = byhost[hh][0]
        near = [o for o in byhost if o != hh and topo.may_write(rep, byhost[o][0])]
        same = [o for o in near if topo.rack(o) == topo.rack(hh)]
        far = [o for o in near if topo.rack(o) != topo.rack(hh)]
        return same[0], far[0]

    h = topo.host(core)
    c = byhost[h].index(core)
    HX, HY = around(h)
    diag = [o for o in byhost if o not in (h, HX, HY)][0]
    h0 = min(byhost)

    def mu(route, hh, i):
        if route == 0:
            return MX[0 if hh in (h0, around(h0)[1]) else 1][i]
        return MY[0 if topo.rack(hh) == topo.rack(h0) else 1][i]

    def xb(k):
        j = T.rank_of(k)
        return T.x[:, j * b:(j + 1) * b]

    def yb(k):
        j = T.rank_of(k)
        return T.y[:, j * b:(j + 1) * b]

    def shares(dsts):
        m = topo.mask(core, dsts[0])
        for d in dsts:
            m &= topo.mask(core, d)
        bits = _bits(m)
        per = 1
        while per * 2 * len(dsts) <= len(bits):
            per *= 2
        return per, [sum(bits[i * per:(i + 1) * per]) for i in range(len(dsts))]

    def send(moves, s):
        per, masks = shares([d for _, d, _ in moves])
        trs = []
        for (src, d, dst), m in zip(moves, masks):
            rid, pid = topo.addr(d, core)
            trs.append(RemoteDMATransfer(dst_ids=[DstId(rid=rid, pnc=pid)], dma_engine_mask=m, remote_sem=sem[s],
                                         src=S[src], dst=S[dst]))
        g.remote_dma_fused(trs, local_sem=sem[s])
        lv[s] += 2 * per * len(moves)

    def signal(dsts, s):
        per, masks = shares(dsts)
        trs = []
        for d, m in zip(dsts, masks):
            rid, pid = topo.addr(d, core)
            trs.append(RemoteDMATransfer(dst_ids=[DstId(rid=rid, pnc=pid)], dma_engine_mask=m, remote_sem=sem[s]))
        g.remote_dma_fused(trs, local_sem=sem[s])
        lv[s] += 2 * per * len(dsts)

    def turn(s, slots, came, go):
        for q, k in zip(queues, (0, 1)):
            q.wait_ge(sem[s], lv[s])
            q.dma_start(yb(came[k]), S[slots[k]]).then_inc(sem[s], 16)
        lv[s] += 32
        for q, k in zip(queues, (0, 1)):
            q.wait_ge(sem[s], lv[s])
            q.dma_start(S[slots[k]], xb(go[k])).then_inc(sem[s], 16)
        lv[s] += 32
        g.wait_ge(sem[s], lv[s])

    def on(d):
        return byhost[h][(c + d) % n]

    plan = []
    for i in range(2):
        w = (byhost[HX][c ^ mu(0, h, i)], byhost[HY][c ^ mu(1, h, i)])
        v = (byhost[diag][c ^ mu(0, h, i) ^ mu(1, diag, i)], byhost[diag][c ^ mu(1, h, i) ^ mu(0, diag, i)])
        u = (byhost[HX][c ^ mu(0, HX, i)], byhost[HY][c ^ mu(1, HY, i)])
        plan.append((w, v, u))

    E, F = [2, 3], [0, 1]
    g.sync.dma_start(S[0], xb(on(1))).then_inc(sem[0], 16)
    g.scalar.dma_start(S[1], xb(on(2))).then_inc(sem[0], 16)
    lv[0] += 32
    g.wait_ge(sem[0], lv[0])
    send([(0, on(1), E[0]), (1, on(2), E[1])], "a")
    g.sync.wait_ge(sem["a"], lv["a"])
    g.sync.dma_start(S[1], xb(on(3))).then_inc(sem["a"], 16)
    lv["a"] += 16
    g.wait_ge(sem["a"], lv["a"])
    send([(1, on(3), 0)], 0)
    for q, k in zip(queues, (0, 1)):
        q.wait_ge(sem["a"], lv["a"])
        q.dma_start(yb((on(-1), on(2))[k]), S[E[k]]).then_inc(sem["a"], 16)
    lv["a"] += 32
    for q, k in zip(queues, (0, 1)):
        q.wait_ge(sem["a"], lv["a"])
        q.dma_start(S[E[k]], xb(plan[0][1][k])).then_inc(sem[1], 16)
    lv[1] += 32
    g.scalar.wait_ge(sem[0], lv[0])
    g.scalar.dma_start(yb(on(1)), S[0]).then_inc(sem["a"], 16)
    lv["a"] += 16
    g.scalar.dma_start(yb(core), xb(core)).then_inc(sem[1], 16)
    lv[1] += 16
    g.wait_ge(sem[0], lv[0])
    g.wait_ge(sem["a"], lv["a"])

    signal(list(plan[0][2]) + list(plan[1][0]), 1)
    for i, (w, v, u) in enumerate(plan):
        p = 1 - i
        g.wait_ge(sem[p], lv[p])
        send([(E[0], w[0], F[0]), (E[1], w[1], F[1])], "a")
        g.wait_ge(sem["a"], lv["a"])
        send([(F[0], u[1], E[1]), (F[1], u[0], E[0])], p)
        turn(p, E, v, w)
        send([(E[0], w[0], F[1]), (E[1], w[1], F[0])], "a")
        turn("a", (F[1], F[0]), u, u)
        send([(F[1], u[0], E[0]), (F[0], u[1], E[1])], p)
        if i + 1 < len(plan):
            g.wait_ge(sem[p], lv[p])
            signal(list(plan[i + 1][2]), 1 - p)
            turn(p, E, w, plan[i + 1][1])
        else:
            for q, k in zip(queues, (0, 1)):
                q.wait_ge(sem[p], lv[p])
                q.dma_start(yb(w[k]), S[E[k]]).then_inc(sem[p], 16)
            lv[p] += 32
            g.wait_ge(sem[p], lv[p])
